import numpy as np
import ml_dtypes


def mxq(x, axis, fmt="e4m3"):
    dtype, down = {"e4m3": (ml_dtypes.float8_e4m3fn, 7), "e5m2": (ml_dtypes.float8_e5m2, 14)}[fmt]
    v = np.moveaxis(np.asarray(x, np.float32).astype(ml_dtypes.bfloat16).astype(np.float64), axis, -1)
    blocks = v.reshape(v.shape[:-1] + (-1, 32))
    amax = np.abs(blocks).max(-1, keepdims=True)
    byte = np.maximum(np.where(amax > 0, np.frexp(amax)[1] - 1 + 127, 0) - down, 1)
    scale = np.exp2(byte - 127.0)
    codes = (blocks / scale).astype(np.float32).astype(dtype).astype(np.float64)
    return np.moveaxis((codes * scale).reshape(v.shape), -1, axis)


WIDE = False


def mx_kscale(k):
    if not WIDE:
        return np.ones(k)
    levels = np.array([10, -10, 5, -5, 0])
    if k % 512:
        return np.exp2(np.random.permutation(np.resize(levels, k // 32))).repeat(32)
    a = np.empty((k // 512, 16))
    for p in range(k // 512):
        a[p, :8] = np.random.permutation(np.resize(levels, 8))
        for g in range(8):
            far = levels[np.abs(levels - a[p, g]) >= 10]
            a[p, g + 8] = far[np.random.randint(len(far))]
    return np.exp2(a.ravel()).repeat(32)


def f64(x):
    return np.asarray(x).astype(np.float64)


def striped(idx):
    return np.tile(idx.reshape(-1, 16).T, (8, 1)).astype(np.uint16)


def unstriped(offs):
    return offs[:16].T.reshape(-1).astype(np.int64)


def striped8(idx):
    return np.concatenate([x.reshape(-1, 16).T for x in idx]).astype(np.uint16)


def runs(offs, k):
    lists = np.stack([offs[16 * r : 16 * r + 16].T.reshape(-1) for r in range(8)]).astype(np.int64)
    return lists[np.arange(k) % 512 // 64]


def pack_weight(w):
    k, n = w.shape
    w = f64(np.asarray(w, np.float32).astype(ml_dtypes.bfloat16)).reshape(k // 32, 32, n)
    amax = np.abs(w).max(1)
    byte = np.clip(np.where(amax > 0, np.frexp(amax)[1] - 1 + 127 - 7, 1), 1, 254)
    scaled = (w * np.exp2(127.0 - byte)[:, None, :]).reshape(k, n).astype(np.float32)
    words = np.ascontiguousarray(scaled.reshape(k // 512, 128, 4, n).transpose(0, 1, 3, 2)).astype(ml_dtypes.float8_e4m3fn).view(np.uint8)
    return words, np.ascontiguousarray(byte.astype(np.uint8).reshape(k // 512, 16, n))


def unpack_weight(words, scales):
    g, p, n, _ = words.shape
    vals = np.ascontiguousarray(words).view(ml_dtypes.float8_e4m3fn).astype(np.float64) * np.repeat(np.exp2(scales.astype(np.float64) - 127.0), 8, axis=1)[..., None]
    return vals.transpose(0, 1, 3, 2).reshape(g * 512, n)

def planes(y):
    n, m = y.shape
    v = y.astype(np.float32).astype(ml_dtypes.bfloat16).astype(np.float64).reshape(n // 32, 32, m)
    top = np.abs(v).max(1)
    byte = np.clip(np.where(top > 0, np.frexp(top)[1] - 1 + 127 - 7, 1), 1, 254)
    codes = (v * np.exp2(127.0 - byte)[:, None, :]).reshape(n, m).astype(np.float32).astype(ml_dtypes.float8_e4m3fn).view(np.uint8)
    words = codes.reshape(n // 512, 128, 4, m).transpose(0, 1, 3, 2)
    return np.ascontiguousarray(words), np.ascontiguousarray(byte.astype(np.uint8).reshape(n // 512, 16, m))


K, T, S, N, H, W = 512, 2048, 512, 512, 512, 256


def setup_inputs():
    n = np.random.standard_normal
    s = mx_kscale(K)[:, None]
    u = mx_kscale(H)
    packed_xT = pack_weight(n((K, T)) * s)
    packed_w3 = pack_weight(n((H, N)) / np.sqrt(H) / u[:, None])
    perm = np.stack([np.random.permutation(S) for _ in range(8)])
    return {
        "x_words": packed_xT[0],
        "x_scales": packed_xT[1],
        "w1": (n((K, H)) / np.sqrt(K) / s * u).astype(np.float32),
        "w2": (n((H, H)) / np.sqrt(H) / u[:, None] * u).astype(np.float32),
        "w3_words": packed_w3[0],
        "w3_scales": packed_w3[1],
        "res": n((N, S)).astype(np.float32),
        "offs": striped(np.random.permutation(T)[:S]),
        "n1": striped8(np.stack([np.random.permutation(S) for _ in range(8)])),
        "n2": striped8(np.stack([np.random.permutation(S) for _ in range(8)])),
        "n3": striped8(perm[:, :W]),
        "n4": striped8(perm[:, W:]),
    }


def reference(x_words, x_scales, w1, w2, w3_words, w3_scales, res, offs, n1, n2, n3, n4):
    xq = unpack_weight(x_words, x_scales)[:, unstriped(offs)]
    y = mxq(f64(w1), 0, "e4m3").T @ xq
    st = y - (y[np.arange(H)[:, None], runs(n1, H)])
    z = np.maximum(st, st[np.arange(H)[:, None], runs(n2, H)])
    h = mxq(f64(w2), 0, "e4m3").T @ mxq(z, 0, "e4m3")
    pa = h[np.arange(H)[:, None], runs(n3, H)]
    pb = h[np.arange(H)[:, None], runs(n4, H)]
    ra = np.maximum(pa, pb)
    z2 = h.copy()
    z2[np.arange(H)[:, None], runs(n3, H)] = ra
    out_0 = f64(res) + (unpack_weight(w3_words, w3_scales).T @ mxq(z2, 0, "e4m3"))
    return (out_0,) + planes(out_0)

from contextlib import ExitStack

import concourse.mybir as mybir

K, T, S, H, N, W = 512, 2048, 512, 512, 512, 256
FLOPS = 2 * S * (K * H + H * H + H * N)

F32 = mybir.dt.float32
BF16 = mybir.dt.bfloat16
I32 = mybir.dt.int32
U32 = mybir.dt.uint32
U16 = mybir.dt.uint16
U8 = mybir.dt.uint8
FP8X4 = mybir.dt.float8_e4m3fn_x4
ALU = mybir.AluOpType

P = 128
PACK = 4
HALF = S // 2
QUARTER = S // 4


def tile_picked_deephopmxfill_none_po_kernel(
    tc, x_words, x_scales, w1, w2, w3_words, w3_scales, res, offs, n1, n2, n3, n4, out_0, out_1, out_2
):
    nc = tc.nc

    with ExitStack() as ctx:
        lists = ctx.enter_context(tc.tile_pool(name="lists", bufs=1))
        keep = ctx.enter_context(tc.tile_pool(name="keep", bufs=1))
        psum = ctx.enter_context(tc.psum_pool(name="psum", bufs=1))

        def sbuf(name, shape, dtype, tag=""):
            return keep.tile(shape, dtype, name=name, tag=tag or name, align_bytes=64)

        def bank(number, name, shape):
            return psum.tile(shape, F32, name=name, tag="bank%d" % number)

        def load_list(name, source):
            tile = lists.tile(list(source.shape), U16, name=name)
            nc.sync.dma_start(tile[:], source)
            return tile

        def entries(tile, first, count):
            return tile[:, first // 16 : (first + count) // 16]

        def load_scale_rows(queue, tile, source):
            for q in range(4):
                queue.dma_start(
                    out=tile[32 * q : 32 * q + 4, :].bitcast(I32), in_=source[0, 4 * q : 4 * q + 4, :].bitcast(I32)
                )

        def words_of(source):
            return source[0].rearrange("p n t -> p (n t)").bitcast(I32)

        def rows_by_four(source):
            return source.rearrange("(p t) c -> p t c", t=PACK)

        def deal_views(grouped, raw, pair):
            dst = grouped[:].rearrange("p (t m j) -> p m j t", t=2, j=PACK)
            src = raw[:].rearrange("p j (m t) -> p m j t", t=PACK)[:, :, :, 2 * pair : 2 * pair + 2]
            return dst, src

        def quantize(codes, scales, values):
            nc.vector.quantize_mx(out=codes.bitcast(FP8X4), scales=scales, in_=values)

        def product(acc, w_codes, w_scales, t, codes, scales):
            cols = slice(P * t, P * (t + 1))
            nc.tensor.matmul_mx(
                out=acc,
                lhsT=w_codes[:, cols].bitcast(FP8X4),
                lhsT_scale=w_scales[:, cols],
                rhs=codes.bitcast(FP8X4),
                rhs_scale=scales,
                start=True,
                stop=True,
            )

        def weave_views(woven, planes):
            dst = woven[:].rearrange("p (c i t) -> p c t i", i=4, t=PACK)
            src = planes.rearrange("p t (c i) -> p c t i", i=4)
            return dst, src

        x_scale_table = sbuf("x_scale_table", [P, T], U8, tag="early")
        nc.vector.memset(x_scale_table[:].bitcast(I32), 0)
        load_scale_rows(nc.scalar, x_scale_table, x_scales)
        offs_t = load_list("offs_t", offs)
        n1_t = load_list("n1_t", n1)
        n2_t = load_list("n2_t", n2)
        w1_raw = sbuf("w1_raw", [P, PACK, H], F32, tag="rows")
        nc.sync.dma_start(out=w1_raw[:], in_=rows_by_four(w1))
        x_word_table = sbuf("x_word_table", [P, T], U32)
        nc.sync.dma_start(out=x_word_table[:].bitcast(I32), in_=words_of(x_words))
        n3_t = load_list("n3_t", n3)
        n4_t = load_list("n4_t", n4)
        w3_scale_raw = sbuf("w3_scale_raw", [P, N], U8)
        nc.vector.memset(w3_scale_raw[:].bitcast(I32), 0)
        load_scale_rows(nc.sync, w3_scale_raw, w3_scales)

        y_win = [sbuf("y_win0", [P, S], F32)] + [sbuf("y_win%d" % t, [P, 2 * S], F32) for t in range(1, PACK)]
        st_win = [sbuf("st_win%d" % t, [P, 2 * S], F32) for t in range(PACK)]
        nc.vector.memset(st_win[PACK - 1][:, S:], 0.0)
        for t in range(2, PACK):
            nc.vector.memset(y_win[t][:, S:], 0.0)
        y_plain = [y_win[1][:, S:]] + [st_win[t - 1][:, S:] for t in range(1, PACK)]

        x_scale = sbuf("x_scale", [P, S], U8)
        nc.vector.tensor_copy(x_scale[:], x_scale_table[:].indirect(offs_t[:]))
        w2_raw = sbuf("w2_raw", [P, PACK, H], F32, tag="early")
        nc.sync.dma_start(out=w2_raw[:], in_=rows_by_four(w2))
        w1_codes = sbuf("w1_codes", [P, H], U32)
        w1_scale = sbuf("w1_scale", [P, H], U8)
        w1_grouped = [sbuf("w1_grouped%d" % pair, [P, 2 * H], BF16) for pair in range(2)]
        nc.vector.tensor_copy(*deal_views(w1_grouped[0], w1_raw, 0))
        nc.scalar.copy(*deal_views(w1_grouped[1], w1_raw, 1))
        for pair in range(2):
            cols = slice(HALF * pair, HALF * (pair + 1))
            quantize(w1_codes[:, cols], w1_scale[:, cols], w1_grouped[pair][:])
        w3_word_raw = sbuf("w3_word_raw", [P, N], U32, tag="w1_grouped0")
        nc.sync.dma_start(out=w3_word_raw[:].bitcast(I32), in_=words_of(w3_words))
        res_t = sbuf("res_t", [P, PACK, S], F32, tag="rows")
        nc.sync.dma_start(out=res_t[:], in_=rows_by_four(res))
        x_codes = sbuf("x_codes", [P, S], U32)
        y_first = []
        for half in range(2):
            cols = slice(HALF * half, HALF * (half + 1))
            nc.vector.tensor_copy(x_codes[:, cols], x_word_table[:].indirect(entries(offs_t, HALF * half, HALF)))
            acc = bank(half, "y0_%d" % half, [P, HALF])
            product(acc[:], w1_codes, w1_scale, 0, x_codes[:, cols], x_scale[:, cols])
            y_first.append(acc)
        y_acc = [None]
        for t in range(1, PACK):
            acc = bank(1 + t, "y%d" % t, [P, S])
            product(acc[:], w1_codes, w1_scale, t, x_codes[:], x_scale[:])
            y_acc.append(acc)

        nc.scalar.copy(y_win[0][:, :HALF], y_first[0][:])
        nc.scalar.copy(y_win[0][:, HALF:], y_first[1][:])
        nc.vector.tensor_copy(y_plain[0][:, :HALF], y_first[0][:])
        nc.scalar.copy(y_plain[0][:, HALF:], y_first[1][:])
        for t in range(1, PACK):
            nc.scalar.copy(y_win[t][:, :S], y_acc[t][:])
            nc.scalar.copy(y_plain[t], y_acc[t][:])

        for half in range(2):
            cols = slice(HALF * half, HALF * (half + 1))
            nc.vector.tensor_tensor(
                st_win[0][:, cols], y_win[0][:].indirect(entries(n1_t, HALF * half, HALF)), y_plain[0][:, cols], ALU.subtract
            )
        picked = sbuf("picked", [P, PACK, S], BF16)

        def fetch_st(t):
            nc.vector.tensor_copy(picked[:, t, :], st_win[t][:].indirect(n2_t[:]))

        for t in range(1, PACK):
            nc.vector.tensor_tensor(st_win[t][:, :S], y_win[t][:].indirect(n1_t[:]), y_plain[t], ALU.subtract)
            fetch_st(t - 1)
        fetch_st(PACK - 1)

        w2_codes = sbuf("w2_codes", [P, H], U32)
        w2_scale = sbuf("w2_scale", [P, H], U8)
        for pair in range(2):
            grouped = sbuf("w2_grouped%d" % pair, [P, 2 * H], BF16)
            nc.scalar.copy(*deal_views(grouped, w2_raw, pair))
            cols = slice(HALF * pair, HALF * (pair + 1))
            quantize(w2_codes[:, cols], w2_scale[:, cols], grouped[:])

        st_round = sbuf("st_round", [P, PACK, S], BF16, tag="early")
        for t in range(PACK):
            nc.scalar.copy(st_round[:, t, :], st_win[t][:, :S])

        quarter = [slice(QUARTER * c, QUARTER * (c + 1)) for c in range(4)]
        z_codes = sbuf("z_codes", [P, S], U32)
        z_scale = sbuf("z_scale", [P, S], U8)
        z_woven = [sbuf("z_woven%d" % c, [P, PACK * QUARTER], BF16) for c in range(4)]
        z_planes = {}
        for first, count in ((0, 1), (2, 2), (1, 1)):
            cols = slice(QUARTER * first, QUARTER * (first + count))
            planes = sbuf("z_planes%d" % first, [P, PACK, QUARTER * count], BF16)
            nc.vector.tensor_tensor(planes[:], st_round[:, :, cols], picked[:, :, cols], ALU.min)
            for c in range(count):
                z_planes[first + c] = planes[:, :, quarter[c]]
        for c in range(2):
            nc.scalar.copy(*weave_views(z_woven[c], z_planes[c]))
        for c in range(2, 4):
            nc.vector.tensor_copy(*weave_views(z_woven[c], z_planes[c]))
        for c in (2, 0, 3, 1):
            quantize(z_codes[:, quarter[c]], z_scale[:, quarter[c]], z_woven[c][:])

        h = [sbuf("h%d" % t, [P, S], F32) for t in range(PACK)]
        pieces = [
            (5, 0, slice(HALF, S)),
            (6, 0, quarter[0]),
            (7, 0, quarter[1]),
            (0, 1, slice(0, S)),
            (1, 2, slice(0, S)),
            (2, 3, slice(0, S)),
        ]
        for number, t, cols in pieces:
            acc = bank(number, "h_acc%d" % number, [P, cols.stop - cols.start])
            product(acc[:], w2_codes, w2_scale, t, z_codes[:, cols], z_scale[:, cols])
            nc.scalar.copy(h[t][:, cols], acc[:])

        w3_codes = sbuf("w3_codes", [P, N], U32, tag="z_woven1")
        w3_scale = sbuf("w3_scale", [P, N], U8, tag="z_woven3")
        nc.vector.tensor_copy(
            w3_scale[:].rearrange("p (t m) -> p t m", t=PACK), w3_scale_raw[:].rearrange("p (m t) -> p t m", t=PACK)
        )
        nc.vector.tensor_copy(
            w3_codes[:].rearrange("p (t m) -> p m t", t=PACK), w3_word_raw[:].rearrange("p (m t) -> p m t", t=PACK)
        )

        pa = sbuf("pa", [P, PACK, W], F32)
        pb = sbuf("pb", [P, PACK, W], F32)
        ra = sbuf("ra", [P, PACK, W], F32)
        z2_woven = [sbuf("z2_woven%d" % c, [P, QUARTER, PACK], BF16) for c in range(4)]

        def fetch_pair(t):
            nc.vector.tensor_copy(pa[:, t, :], h[t][:].indirect(n3_t[:]))
            nc.vector.tensor_copy(pb[:, t, :], h[t][:].indirect(n4_t[:]))

        def larger(t):
            nc.vector.tensor_tensor(ra[:, t, :], pa[:, t, :], pb[:, t, :], ALU.min)

        def put_back(t):
            nc.vector.tensor_copy(h[t][:].indirect(n3_t[:]), ra[:, t, :])
            for c in range(4):
                nc.scalar.copy(z2_woven[c][:, :, t], h[t][:, QUARTER * c : QUARTER * (c + 1)])

        fetch_pair(0)
        fetch_pair(1)
        larger(0)
        fetch_pair(2)
        put_back(0)
        larger(1)
        fetch_pair(3)
        put_back(1)
        larger(2)
        larger(3)
        put_back(2)
        put_back(3)

        out_codes = sbuf("out_codes", [P, S], U32)
        out_scale = sbuf("out_scale", [P, S], U8)
        out_rows = rows_by_four(out_0)
        out_words = words_of(out_1)
        accs, sums, woven = [], [], []

        def multiply(c):
            codes = sbuf("z2_codes%d" % c, [P, QUARTER], U32)
            scales = sbuf("z2_scale%d" % c, [P, QUARTER], U8)
            quantize(codes[:], scales[:], z2_woven[c][:].rearrange("p j t -> p (j t)"))
            acc = bank((3 + c) % 8, "out_acc%d" % c, [P, PACK, QUARTER])
            for t in range(PACK):
                product(acc[:, t, :], w3_codes, w3_scale, t, codes[:], scales[:])
            accs.append(acc)

        def add_residual(c):
            cols = slice(QUARTER * c, QUARTER * (c + 1))
            total = sbuf("total%d" % c, [P, PACK, QUARTER], F32)
            nc.vector.tensor_tensor(total[:], res_t[:, :, cols], accs[c][:], ALU.subtract)
            nc.sync.dma_start(out=out_rows[:, :, cols], in_=total[:])
            rounded = sbuf("rounded%d" % c, [P, PACK * QUARTER], BF16)
            if c < 3:
                nc.scalar.copy(*weave_views(rounded, total[:]))
            else:
                nc.vector.tensor_copy(*weave_views(rounded, total[:]))
            woven.append(rounded)

        def hand_on(c):
            cols = slice(QUARTER * c, QUARTER * (c + 1))
            quantize(out_codes[:, cols], out_scale[:, cols], woven[c][:])
            if c % 2 == 1:
                both = slice(QUARTER * (c - 1), QUARTER * (c + 1))
                nc.sync.dma_start(out=out_words[:, both], in_=out_codes[:, both].bitcast(I32))

        multiply(0)
        multiply(1)
        add_residual(0)
        multiply(2)
        add_residual(1)
        multiply(3)
        add_residual(2)
        hand_on(0)
        hand_on(1)
        add_residual(3)
        hand_on(2)
        hand_on(3)
        for q in range(4):
            queue = nc.scalar if q % 2 == 0 else nc.sync
            queue.dma_start(
                out=out_2[0, 4 * q : 4 * q + 4, :].bitcast(I32), in_=out_scale[32 * q : 32 * q + 4, :].bitcast(I32)
            )
